import numpy as np, ml_dtypes
CORES = [15,47,79,175,207]
N = 5
TK = 512
def setup_inputs(rng):
    return {"c": rng.standard_normal((N, 128, 128), dtype=np.float32).astype(ml_dtypes.bfloat16), "x": rng.standard_normal((N, 128, TK), dtype=np.float32).astype(ml_dtypes.bfloat16)}
def setup_inputs_big(rng):
    d = setup_inputs(rng)
    for k in ("c", "x"): d[k] = (d[k].astype(np.float32) * 1024.0).astype(d[k].dtype)
    return d
def setup_inputs_small(rng):
    d = setup_inputs(rng)
    for k in ("c", "x"): d[k] = (d[k].astype(np.float32) * (1 / 1024.0)).astype(d[k].dtype)
    return d
def setup_inputs_apart(rng):
    d = setup_inputs(rng)
    f = (10.0 ** rng.permutation(np.linspace(-1.5, 1.5, N))).astype(np.float32).reshape(N, 1, 1)
    for k in ("c", "x"): d[k] = (d[k].astype(np.float32) * f).astype(d[k].dtype)
    return d
def reference(c, x):
    C, X = c.astype(np.float64), x.astype(np.float64)
    y = np.zeros((N, 128, TK))
    for r in range(N):
        for j in range(N):
            y[r] += C[(r - j) % N].T @ X[j]
    return {"y": y.astype(ml_dtypes.bfloat16 if x.dtype != np.float64 else np.float64)}

@@ -1,0 +1,97 @@
+N = 5
+CW = 128
+XW = 512
+BW = CW + XW
+HALF = XW // 2
+
+SCRATCH = {
+    "own": ("sbuf", [128, BW], "bfloat16"),
+    "land": ("sbuf", [128, (N - 1) * BW], "bfloat16"),
+    "out": ("sbuf", [128, XW], "bfloat16"),
+    "acc0": ("psum", [128, 512], "float32"),
+    "acc1": ("psum", [128, 512], "float32"),
+}
+SEMAPHORES = ["ld", "arr1", "arr2", "arr3", "arr4", "sent", "mm0", "mm1", "cp0", "cp1", "st0", "st1"]
+
+
+def _engines(mask):
+    bits = [b for b in range(16) if (mask >> b) & 1]
+    n = 1
+    while n * 2 <= len(bits):
+        n *= 2
+    use = bits[:n]
+    m = 0
+    for b in use:
+        m |= 1 << b
+    return m, n
+
+
+def rank_program(g, core, T, topo):
+    r = T.rank_of(core)
+    if r is None:
+        return
+    sem = T.sem
+
+    g.sync.dma_start(T.own[:, CW:BW], T.x[:]).then_inc(sem.ld, 16)
+    g.scalar.dma_start(T.own[:, 0:CW], T.c[:]).then_inc(sem.ld, 16)
+
+    g.wait_ge(sem.ld, 32)
+    sent = 0
+    n_in = {}
+    for t in range(1, N):
+        dst = T.cores[(r + t) % N]
+        rid, pid = topo.addr(dst, core)
+        m, n = _engines(topo.mask(core, dst))
+        g.remote_dma(out_ap=T.land[:, (t - 1) * BW:t * BW], in_ap=T.own[:], remote_sem=sem["arr%d" % t],
+                     local_sem=sem.sent, pid=pid, routing_id=rid, dma_engine_mask=m)
+        sent += n
+        src = T.cores[(r - t) % N]
+        n_in[t] = _engines(topo.mask(src, core))[1]
+
+    def block(q):
+        t = (r - q) % N
+        return (T.own, 0) if t == 0 else (T.land, (t - 1) * BW)
+
+    pairs = sorted((max((r - k) % N, k), k, (r - k) % N) for k in range(N))
+    acc = [T.acc0, T.acc1]
+    mm = [sem.mm0, sem.mm1]
+    g.tensor.wait_ge(sem.ld, 32)
+    last_step = pairs[-1][0]
+    waited = 0
+
+    def product(h, i):
+        _, k, j = pairs[i]
+        cb, co = block(k)
+        xb, xo = block(j)
+        return g.tensor.matmul(acc[h][:, 0:HALF], cb[:, co:co + CW], xb[:, xo + CW + h * HALF:xo + CW + (h + 1) * HALF],
+                               i == 0, i == N - 1)
+
+    early = [i for i in range(N) if pairs[i][0] < last_step]
+    late = [i for i in range(N) if pairs[i][0] == last_step]
+    for i in early:
+        while waited < pairs[i][0]:
+            waited += 1
+            g.tensor.wait_ge(sem["arr%d" % waited], n_in[waited])
+        product(0, i)
+        product(1, i)
+    while waited < N - 1:
+        waited += 1
+        g.tensor.wait_ge(sem["arr%d" % waited], n_in[waited])
+    for h in range(2):
+        for i in late:
+            ins = product(h, i)
+        ins.then_inc(mm[h], 1)
+
+    g.vector.wait_ge(sem.mm0, 1)
+    g.vector.tensor_copy(T.out[:, 0:HALF], T.acc0[:, 0:HALF]).then_inc(sem.cp0, 1)
+    g.vector.wait_ge(sem.mm1, 1)
+    g.vector.tensor_copy(T.out[:, HALF:XW], T.acc1[:, 0:HALF]).then_inc(sem.cp1, 1)
+
+    g.sync.wait_ge(sem.cp0, 1)
+    g.sync.dma_start(T.y[:, 0:HALF], T.out[:, 0:HALF]).then_inc(sem.st0, 16)
+    g.sync.wait_ge(sem.st0, 16)
+    g.scalar.wait_ge(sem.cp1, 1)
+    g.scalar.dma_start(T.y[:, HALF:XW], T.out[:, HALF:XW]).then_inc(sem.st1, 16)
+    g.scalar.wait_ge(sem.st1, 16)
+
+    g.wait_ge(sem.sent, sent)

@@ -3,6 +3,8 @@ CW = 128
 XW = 512
 BW = CW + XW
 HALF = XW // 2
+DIRECT = [1, 2, 3]
+RELAYED = 4
 
 SCRATCH = {
     "own": ("sbuf", [128, BW], "bfloat16"),
@@ -11,7 +13,8 @@ SCRATCH = {
     "acc0": ("psum", [128, 512], "float32"),
     "acc1": ("psum", [128, 512], "float32"),
 }
-SEMAPHORES = ["ld", "arr1", "arr2", "arr3", "arr4", "sent", "mm0", "mm1", "cp0", "cp1", "st0", "st1"]
+SEMAPHORES = ["ldc", "ldx", "hc", "hx", "a1", "a2", "a3", "a4c", "a4x", "sent",
+              "mm0", "mm1", "cp0", "cp1", "st0", "st1"]
 
 
 def _engines(mask):
@@ -19,68 +22,111 @@ def _engines(mask):
     n = 1
     while n * 2 <= len(bits):
         n *= 2
-    use = bits[:n]
     m = 0
-    for b in use:
+    for b in bits[:n]:
         m |= 1 << b
     return m, n
 
 
+def _relay(topo, T, s):
+    c = T.cores[s]
+    w = topo.CORES_PER_CHIP
+    for q in range(max(0, c - w + 1), c + w):
+        if (topo.host(q) == topo.host(c) and topo.chip(q) == topo.chip(c) and topo.die(q) != topo.die(c)
+                and topo.may_write(q, T.cores[(s + RELAYED) % N])):
+            return q
+    return None
+
+
+def _hand_over_mask(topo, T, s):
+    c = T.cores[s]
+    off = topo.mask(c, T.cores[(s + 1) % N])
+    return _engines(topo.mask(c, _relay(topo, T, s)) & ~off)
+
+
+def _write(g, core, T, topo, dst, out_ap, in_ap, rs, mask=None):
+    rid, pid = topo.addr(dst, core)
+    m, n = _engines(topo.mask(core, dst)) if mask is None else mask
+    g.remote_dma(out_ap=out_ap, in_ap=in_ap, remote_sem=rs, local_sem=T.sem.sent, pid=pid, routing_id=rid,
+                 dma_engine_mask=m)
+    return n
+
+
+def _relay_program(g, core, T, topo, s):
+    sem = T.sem
+    n_h = _hand_over_mask(topo, T, s)[1]
+    dst = T.cores[(s + RELAYED) % N]
+    o = (RELAYED - 1) * BW
+    g.wait_ge(sem.hc, n_h)
+    sent = _write(g, core, T, topo, dst, T.land[:, o:o + CW], T.own[:, 0:CW], sem.a4c)
+    g.wait_ge(sem.hx, n_h)
+    sent += _write(g, core, T, topo, dst, T.land[:, o + CW:o + BW], T.own[:, CW:BW], sem.a4x)
+    g.wait_ge(sem.sent, sent)
+
+
 def rank_program(g, core, T, topo):
     r = T.rank_of(core)
-    if r is None:
-        return
     sem = T.sem
+    if r is None:
+        for s in range(N):
+            if _relay(topo, T, s) == core:
+                _relay_program(g, core, T, topo, s)
+        return
 
-    g.sync.dma_start(T.own[:, CW:BW], T.x[:]).then_inc(sem.ld, 16)
-    g.scalar.dma_start(T.own[:, 0:CW], T.c[:]).then_inc(sem.ld, 16)
+    g.scalar.dma_start(T.own[:, 0:CW], T.c[:]).then_inc(sem.ldc, 16)
+    g.sync.dma_start(T.own[:, CW:BW], T.x[:]).then_inc(sem.ldx, 16)
 
-    g.wait_ge(sem.ld, 32)
-    sent = 0
-    n_in = {}
-    for t in range(1, N):
-        dst = T.cores[(r + t) % N]
-        rid, pid = topo.addr(dst, core)
-        m, n = _engines(topo.mask(core, dst))
-        g.remote_dma(out_ap=T.land[:, (t - 1) * BW:t * BW], in_ap=T.own[:], remote_sem=sem["arr%d" % t],
-                     local_sem=sem.sent, pid=pid, routing_id=rid, dma_engine_mask=m)
-        sent += n
-        src = T.cores[(r - t) % N]
-        n_in[t] = _engines(topo.mask(src, core))[1]
+    rel = _relay(topo, T, r)
+    hm = _hand_over_mask(topo, T, r)
+    g.wait_ge(sem.ldc, 16)
+    sent = _write(g, core, T, topo, rel, T.own[:, 0:CW], T.own[:, 0:CW], sem.hc, hm)
+    g.wait_ge(sem.ldx, 16)
+    sent += _write(g, core, T, topo, rel, T.own[:, CW:BW], T.own[:, CW:BW], sem.hx, hm)
+    for t in DIRECT:
+        sent += _write(g, core, T, topo, T.cores[(r + t) % N], T.land[:, (t - 1) * BW:t * BW], T.own[:], sem["a%d" % t])
+
+    def n_direct(t):
+        return _engines(topo.mask(T.cores[(r - t) % N], core))[1]
+
+    n_rel = _engines(topo.mask(_relay(topo, T, (r - RELAYED) % N), core))[1]
+    events = [[(sem.ldc, 16), (sem.ldx, 16)],
+              [(sem.a4c, n_rel)],
+              [(sem.a1, n_direct(1))],
+              [(sem.a2, n_direct(2))],
+              [(sem.a4x, n_rel)],
+              [(sem.a3, n_direct(3))]]
+    c_event = {0: 0, 4: 1, 1: 2, 2: 3, 3: 5}
+    x_event = {0: 0, 1: 2, 2: 3, 4: 4, 3: 5}
 
     def block(q):
         t = (r - q) % N
         return (T.own, 0) if t == 0 else (T.land, (t - 1) * BW)
 
-    pairs = sorted((max((r - k) % N, k), k, (r - k) % N) for k in range(N))
+    pairs = sorted((max(c_event[(r - k) % N], x_event[k]), k, (r - k) % N) for k in range(N))
     acc = [T.acc0, T.acc1]
     mm = [sem.mm0, sem.mm1]
-    g.tensor.wait_ge(sem.ld, 32)
-    last_step = pairs[-1][0]
-    waited = 0
+    last = len(events) - 1
 
     def product(h, i):
         _, k, j = pairs[i]
         cb, co = block(k)
         xb, xo = block(j)
-        return g.tensor.matmul(acc[h][:, 0:HALF], cb[:, co:co + CW], xb[:, xo + CW + h * HALF:xo + CW + (h + 1) * HALF],
-                               i == 0, i == N - 1)
+        lo = xo + CW + h * HALF
+        return g.tensor.matmul(acc[h][:, 0:HALF], cb[:, co:co + CW], xb[:, lo:lo + HALF], i == 0, i == N - 1)
 
-    early = [i for i in range(N) if pairs[i][0] < last_step]
-    late = [i for i in range(N) if pairs[i][0] == last_step]
-    for i in early:
-        while waited < pairs[i][0]:
-            waited += 1
-            g.tensor.wait_ge(sem["arr%d" % waited], n_in[waited])
-        product(0, i)
-        product(1, i)
-    while waited < N - 1:
-        waited += 1
-        g.tensor.wait_ge(sem["arr%d" % waited], n_in[waited])
-    for h in range(2):
-        for i in late:
-            ins = product(h, i)
-        ins.then_inc(mm[h], 1)
+    for e in range(last + 1):
+        for s_, n_ in events[e]:
+            g.tensor.wait_ge(s_, n_)
+        todo = [i for i in range(N) if pairs[i][0] == e]
+        if e < last:
+            for i in todo:
+                product(0, i)
+                product(1, i)
+        else:
+            for h in range(2):
+                for i in todo:
+                    ins = product(h, i)
+                ins.then_inc(mm[h], 1)
 
     g.vector.wait_ge(sem.mm0, 1)
     g.vector.tensor_copy(T.out[:, 0:HALF], T.acc0[:, 0:HALF]).then_inc(sem.cp0, 1)

@@ -1,47 +1,65 @@
+from concourse.bass import DstId, RemoteDMATransfer
+
 N = 5
 CW = 128
 XW = 512
 BW = CW + XW
 HALF = XW // 2
-DIRECT = [1, 2, 3]
 RELAYED = 4
+CARRIED = 3
 
 SCRATCH = {
     "own": ("sbuf", [128, BW], "bfloat16"),
+    "cd": ("dram", [128, CW], "bfloat16"),
     "land": ("sbuf", [128, (N - 1) * BW], "bfloat16"),
     "out": ("sbuf", [128, XW], "bfloat16"),
     "acc0": ("psum", [128, 512], "float32"),
     "acc1": ("psum", [128, 512], "float32"),
 }
-SEMAPHORES = ["ldc", "ldx", "hc", "hx", "a1", "a2", "a3", "a4c", "a4x", "sent",
+SEMAPHORES = ["ldd", "ldc", "ldx", "hc", "hx0", "hx1", "a1", "a2", "a3", "a3c", "a4c", "a4x0", "a4x1", "sent",
               "mm0", "mm1", "cp0", "cp1", "st0", "st1"]
 
 
+def _bits(mask):
+    return [b for b in range(16) if (mask >> b) & 1]
+
+
+def _mask_of(bits):
+    m = 0
+    for b in bits:
+        m |= 1 << b
+    return m
+
+
 def _engines(mask):
-    bits = [b for b in range(16) if (mask >> b) & 1]
+    bits = _bits(mask)
     n = 1
     while n * 2 <= len(bits):
         n *= 2
-    m = 0
-    for b in bits[:n]:
-        m |= 1 << b
-    return m, n
+    return _mask_of(bits[:n]), n
 
 
-def _relay(topo, T, s):
+def _helpers(topo, T, s):
     c = T.cores[s]
     w = topo.CORES_PER_CHIP
+    found = []
     for q in range(max(0, c - w + 1), c + w):
         if (topo.host(q) == topo.host(c) and topo.chip(q) == topo.chip(c) and topo.die(q) != topo.die(c)
-                and topo.may_write(q, T.cores[(s + RELAYED) % N])):
-            return q
-    return None
+                and topo.may_write(q, T.cores[(s + RELAYED) % N]) and topo.may_write(q, T.cores[(s + CARRIED) % N])):
+            found.append(q)
+    return found[0], found[1]
 
 
 def _hand_over_mask(topo, T, s):
     c = T.cores[s]
     off = topo.mask(c, T.cores[(s + 1) % N])
-    return _engines(topo.mask(c, _relay(topo, T, s)) & ~off)
+    return _engines(topo.mask(c, _helpers(topo, T, s)[0]) & ~off)
+
+
+def _two_parts(mn):
+    bits = _bits(mn[0])
+    h = len(bits) // 2
+    return (_mask_of(bits[:h]), h), (_mask_of(bits[h:]), h)
 
 
 def _write(g, core, T, topo, dst, out_ap, in_ap, rs, mask=None):
@@ -54,13 +72,25 @@ def _write(g, core, T, topo, dst, out_ap, in_ap, rs, mask=None):
 
 def _relay_program(g, core, T, topo, s):
     sem = T.sem
-    n_h = _hand_over_mask(topo, T, s)[1]
+    hm = _hand_over_mask(topo, T, s)
     dst = T.cores[(s + RELAYED) % N]
     o = (RELAYED - 1) * BW
-    g.wait_ge(sem.hc, n_h)
-    sent = _write(g, core, T, topo, dst, T.land[:, o:o + CW], T.own[:, 0:CW], sem.a4c)
-    g.wait_ge(sem.hx, n_h)
-    sent += _write(g, core, T, topo, dst, T.land[:, o + CW:o + BW], T.own[:, CW:BW], sem.a4x)
+    g.wait_ge(sem.hc, _two_parts(hm)[0][1])
+    sent = _write(g, core, T, topo, dst, T.land[:, o:o + CW], T.cd[:], sem.a4c)
+    g.wait_ge(sem.hx0, hm[1])
+    sent += _write(g, core, T, topo, dst, T.land[:, o + CW:o + CW + HALF], T.own[:, CW:CW + HALF], sem.a4x0)
+    g.wait_ge(sem.hx1, hm[1])
+    sent += _write(g, core, T, topo, dst, T.land[:, o + CW + HALF:o + BW], T.own[:, CW + HALF:BW], sem.a4x1)
+    g.wait_ge(sem.sent, sent)
+
+
+def _carrier_program(g, core, T, topo, s):
+    sem = T.sem
+    hm = _hand_over_mask(topo, T, s)
+    dst = T.cores[(s + CARRIED) % N]
+    o = (CARRIED - 1) * BW
+    g.wait_ge(sem.hc, _two_parts(hm)[1][1])
+    sent = _write(g, core, T, topo, dst, T.land[:, o:o + CW], T.cd[:], sem.a3c)
     g.wait_ge(sem.sent, sent)
 
 
@@ -69,63 +99,77 @@ def rank_program(g, core, T, topo):
     sem = T.sem
     if r is None:
         for s in range(N):
-            if _relay(topo, T, s) == core:
+            rel_s, car_s = _helpers(topo, T, s)
+            if rel_s == core:
                 _relay_program(g, core, T, topo, s)
+            elif car_s == core:
+                _carrier_program(g, core, T, topo, s)
         return
 
+    g.scalar.dma_start(T.cd[:], T.c[:]).then_inc(sem.ldd, 16)
     g.scalar.dma_start(T.own[:, 0:CW], T.c[:]).then_inc(sem.ldc, 16)
     g.sync.dma_start(T.own[:, CW:BW], T.x[:]).then_inc(sem.ldx, 16)
 
-    rel = _relay(topo, T, r)
+    rel, car = _helpers(topo, T, r)
     hm = _hand_over_mask(topo, T, r)
-    g.wait_ge(sem.ldc, 16)
-    sent = _write(g, core, T, topo, rel, T.own[:, 0:CW], T.own[:, 0:CW], sem.hc, hm)
+    g.wait_ge(sem.ldd, 16)
+    trs = []
+    sent = 0
+    for dst, (m, n) in zip((rel, car), _two_parts(hm)):
+        rid, pid = topo.addr(dst, core)
+        trs.append(RemoteDMATransfer(dst_ids=[DstId(rid=rid, pnc=pid)], dma_engine_mask=m, remote_sem=sem.hc,
+                                     src=T.cd[:], dst=T.cd[:]))
+        sent += n
+    g.remote_dma_fused(trs, local_sem=sem.sent)
+
+    def slot(t):
+        return (t - 1) * BW
+
     g.wait_ge(sem.ldx, 16)
-    sent += _write(g, core, T, topo, rel, T.own[:, CW:BW], T.own[:, CW:BW], sem.hx, hm)
-    for t in DIRECT:
-        sent += _write(g, core, T, topo, T.cores[(r + t) % N], T.land[:, (t - 1) * BW:t * BW], T.own[:], sem["a%d" % t])
+    sent += _write(g, core, T, topo, rel, T.own[:, CW:CW + HALF], T.own[:, CW:CW + HALF], sem.hx0, hm)
+    g.wait_ge(sem.ldc, 16)
+    sent += _write(g, core, T, topo, T.cores[(r + 1) % N], T.land[:, slot(1):slot(1) + BW], T.own[:], sem.a1)
+    sent += _write(g, core, T, topo, rel, T.own[:, CW + HALF:BW], T.own[:, CW + HALF:BW], sem.hx1, hm)
+    sent += _write(g, core, T, topo, T.cores[(r + 2) % N], T.land[:, slot(2):slot(2) + BW], T.own[:], sem.a2)
+    sent += _write(g, core, T, topo, T.cores[(r + 3) % N], T.land[:, slot(3) + CW:slot(3) + BW], T.own[:, CW:BW], sem.a3)
 
-    def n_direct(t):
-        return _engines(topo.mask(T.cores[(r - t) % N], core))[1]
+    def n_from(q):
+        return _engines(topo.mask(q, core))[1]
 
-    n_rel = _engines(topo.mask(_relay(topo, T, (r - RELAYED) % N), core))[1]
+    n_rel = n_from(_helpers(topo, T, (r - RELAYED) % N)[0])
+    n_car = n_from(_helpers(topo, T, (r - CARRIED) % N)[1])
     events = [[(sem.ldc, 16), (sem.ldx, 16)],
               [(sem.a4c, n_rel)],
-              [(sem.a1, n_direct(1))],
-              [(sem.a2, n_direct(2))],
-              [(sem.a4x, n_rel)],
-              [(sem.a3, n_direct(3))]]
-    c_event = {0: 0, 4: 1, 1: 2, 2: 3, 3: 5}
-    x_event = {0: 0, 1: 2, 2: 3, 4: 4, 3: 5}
+              [(sem.a3c, n_car)],
+              [(sem.a1, n_from(T.cores[(r - 1) % N]))],
+              [(sem.a2, n_from(T.cores[(r - 2) % N]))],
+              [(sem.a4x0, n_rel)],
+              [(sem.a4x1, n_rel)],
+              [(sem.a3, n_from(T.cores[(r - 3) % N]))]]
+    c_event = {0: 0, 4: 1, 3: 2, 1: 3, 2: 4}
+    x_event = {0: (0, 0), 1: (3, 3), 2: (4, 4), 4: (5, 6), 3: (7, 7)}
 
     def block(q):
         t = (r - q) % N
-        return (T.own, 0) if t == 0 else (T.land, (t - 1) * BW)
+        return (T.own, 0) if t == 0 else (T.land, slot(t))
 
-    pairs = sorted((max(c_event[(r - k) % N], x_event[k]), k, (r - k) % N) for k in range(N))
+    tasks = sorted((max(c_event[(r - k) % N], x_event[k][h]), k, h) for k in range(N) for h in range(2))
     acc = [T.acc0, T.acc1]
     mm = [sem.mm0, sem.mm1]
-    last = len(events) - 1
-
-    def product(h, i):
-        _, k, j = pairs[i]
-        cb, co = block(k)
-        xb, xo = block(j)
-        lo = xo + CW + h * HALF
-        return g.tensor.matmul(acc[h][:, 0:HALF], cb[:, co:co + CW], xb[:, lo:lo + HALF], i == 0, i == N - 1)
-
-    for e in range(last + 1):
+    done = [0, 0]
+    for e in range(len(events)):
         for s_, n_ in events[e]:
             g.tensor.wait_ge(s_, n_)
-        todo = [i for i in range(N) if pairs[i][0] == e]
-        if e < last:
-            for i in todo:
-                product(0, i)
-                product(1, i)
-        else:
-            for h in range(2):
-                for i in todo:
-                    ins = product(h, i)
+        for ev, k, h in tasks:
+            if ev != e:
+                continue
+            cb, co = block(k)
+            xb, xo = block((r - k) % N)
+            lo = xo + CW + h * HALF
+            ins = g.tensor.matmul(acc[h][:, 0:HALF], cb[:, co:co + CW], xb[:, lo:lo + HALF], done[h] == 0,
+                                  done[h] == N - 1)
+            done[h] += 1
+            if done[h] == N:
                 ins.then_inc(mm[h], 1)
 
     g.vector.wait_ge(sem.mm0, 1)

from concourse.bass import DstId, RemoteDMATransfer

N = 5
CW = 128
XW = 512
BW = CW + XW
HALF = XW // 2
RELAYED = 4
CARRIED = 3

SCRATCH = {
    "own": ("sbuf", [128, BW], "bfloat16"),
    "cd": ("dram", [128, CW], "bfloat16"),
    "land": ("sbuf", [128, (N - 1) * BW], "bfloat16"),
    "out": ("sbuf", [128, XW], "bfloat16"),
    "acc0": ("psum", [128, 512], "float32"),
    "acc1": ("psum", [128, 512], "float32"),
}
SEMAPHORES = ["ldd", "ldc", "ldx", "hc", "hx0", "hx1", "a1", "a2", "a3", "a3c", "a4c", "a4x0", "a4x1", "sent",
              "mm0", "mm1", "cp0", "cp1", "st0", "st1"]


def _bits(mask):
    return [b for b in range(16) if (mask >> b) & 1]


def _mask_of(bits):
    m = 0
    for b in bits:
        m |= 1 << b
    return m


def _engines(mask):
    bits = _bits(mask)
    n = 1
    while n * 2 <= len(bits):
        n *= 2
    return _mask_of(bits[:n]), n


def _helpers(topo, T, s):
    c = T.cores[s]
    w = topo.CORES_PER_CHIP
    found = []
    for q in range(max(0, c - w + 1), c + w):
        if (topo.host(q) == topo.host(c) and topo.chip(q) == topo.chip(c) and topo.die(q) != topo.die(c)
                and topo.may_write(q, T.cores[(s + RELAYED) % N]) and topo.may_write(q, T.cores[(s + CARRIED) % N])):
            found.append(q)
    return found[0], found[1]


def _hand_over_mask(topo, T, s):
    c = T.cores[s]
    off = topo.mask(c, T.cores[(s + 1) % N])
    return _engines(topo.mask(c, _helpers(topo, T, s)[0]) & ~off)


def _two_parts(mn):
    bits = _bits(mn[0])
    h = len(bits) // 2
    return (_mask_of(bits[:h]), h), (_mask_of(bits[h:]), h)


def _write(g, core, T, topo, dst, out_ap, in_ap, rs, mask=None):
    rid, pid = topo.addr(dst, core)
    m, n = _engines(topo.mask(core, dst)) if mask is None else mask
    g.remote_dma(out_ap=out_ap, in_ap=in_ap, remote_sem=rs, local_sem=T.sem.sent, pid=pid, routing_id=rid,
                 dma_engine_mask=m)
    return n


def _relay_program(g, core, T, topo, s):
    sem = T.sem
    hm = _hand_over_mask(topo, T, s)
    dst = T.cores[(s + RELAYED) % N]
    o = (RELAYED - 1) * BW
    g.wait_ge(sem.hc, _two_parts(hm)[0][1])
    sent = _write(g, core, T, topo, dst, T.land[:, o:o + CW], T.cd[:], sem.a4c)
    g.wait_ge(sem.hx0, hm[1])
    sent += _write(g, core, T, topo, dst, T.land[:, o + CW:o + CW + HALF], T.own[:, CW:CW + HALF], sem.a4x0)
    g.wait_ge(sem.hx1, hm[1])
    sent += _write(g, core, T, topo, dst, T.land[:, o + CW + HALF:o + BW], T.own[:, CW + HALF:BW], sem.a4x1)
    g.wait_ge(sem.sent, sent)


def _carrier_program(g, core, T, topo, s):
    sem = T.sem
    hm = _hand_over_mask(topo, T, s)
    dst = T.cores[(s + CARRIED) % N]
    o = (CARRIED - 1) * BW
    g.wait_ge(sem.hc, _two_parts(hm)[1][1])
    sent = _write(g, core, T, topo, dst, T.land[:, o:o + CW], T.cd[:], sem.a3c)
    g.wait_ge(sem.sent, sent)


def rank_program(g, core, T, topo):
    r = T.rank_of(core)
    sem = T.sem
    if r is None:
        for s in range(N):
            rel_s, car_s = _helpers(topo, T, s)
            if rel_s == core:
                _relay_program(g, core, T, topo, s)
            elif car_s == core:
                _carrier_program(g, core, T, topo, s)
        return

    g.scalar.dma_start(T.cd[:], T.c[:]).then_inc(sem.ldd, 16)
    g.scalar.dma_start(T.own[:, 0:CW], T.c[:]).then_inc(sem.ldc, 16)
    g.sync.dma_start(T.own[:, CW:BW], T.x[:]).then_inc(sem.ldx, 16)

    rel, car = _helpers(topo, T, r)
    hm = _hand_over_mask(topo, T, r)
    g.wait_ge(sem.ldd, 16)
    trs = []
    sent = 0
    for dst, (m, n) in zip((rel, car), _two_parts(hm)):
        rid, pid = topo.addr(dst, core)
        trs.append(RemoteDMATransfer(dst_ids=[DstId(rid=rid, pnc=pid)], dma_engine_mask=m, remote_sem=sem.hc,
                                     src=T.cd[:], dst=T.cd[:]))
        sent += n
    g.remote_dma_fused(trs, local_sem=sem.sent)

    def slot(t):
        return (t - 1) * BW

    g.wait_ge(sem.ldx, 16)
    sent += _write(g, core, T, topo, rel, T.own[:, CW:CW + HALF], T.own[:, CW:CW + HALF], sem.hx0, hm)
    g.wait_ge(sem.ldc, 16)
    sent += _write(g, core, T, topo, T.cores[(r + 1) % N], T.land[:, slot(1):slot(1) + BW], T.own[:], sem.a1)
    sent += _write(g, core, T, topo, rel, T.own[:, CW + HALF:BW], T.own[:, CW + HALF:BW], sem.hx1, hm)
    sent += _write(g, core, T, topo, T.cores[(r + 2) % N], T.land[:, slot(2):slot(2) + BW], T.own[:], sem.a2)
    sent += _write(g, core, T, topo, T.cores[(r + 3) % N], T.land[:, slot(3) + CW:slot(3) + BW], T.own[:, CW:BW], sem.a3)

    def n_from(q):
        return _engines(topo.mask(q, core))[1]

    n_rel = n_from(_helpers(topo, T, (r - RELAYED) % N)[0])
    n_car = n_from(_helpers(topo, T, (r - CARRIED) % N)[1])
    events = [[(sem.ldc, 16), (sem.ldx, 16)],
              [(sem.a4c, n_rel)],
              [(sem.a3c, n_car)],
              [(sem.a1, n_from(T.cores[(r - 1) % N]))],
              [(sem.a2, n_from(T.cores[(r - 2) % N]))],
              [(sem.a4x0, n_rel)],
              [(sem.a4x1, n_rel)],
              [(sem.a3, n_from(T.cores[(r - 3) % N]))]]
    c_event = {0: 0, 4: 1, 3: 2, 1: 3, 2: 4}
    x_event = {0: (0, 0), 1: (3, 3), 2: (4, 4), 4: (5, 6), 3: (7, 7)}

    def block(q):
        t = (r - q) % N
        return (T.own, 0) if t == 0 else (T.land, slot(t))

    tasks = sorted((max(c_event[(r - k) % N], x_event[k][h]), k, h) for k in range(N) for h in range(2))
    acc = [T.acc0, T.acc1]
    mm = [sem.mm0, sem.mm1]
    done = [0, 0]
    for e in range(len(events)):
        for s_, n_ in events[e]:
            g.tensor.wait_ge(s_, n_)
        for ev, k, h in tasks:
            if ev != e:
                continue
            cb, co = block(k)
            xb, xo = block((r - k) % N)
            lo = xo + CW + h * HALF
            ins = g.tensor.matmul(acc[h][:, 0:HALF], cb[:, co:co + CW], xb[:, lo:lo + HALF], done[h] == 0,
                                  done[h] == N - 1)
            done[h] += 1
            if done[h] == N:
                ins.then_inc(mm[h], 1)

    g.vector.wait_ge(sem.mm0, 1)
    g.vector.tensor_copy(T.out[:, 0:HALF], T.acc0[:, 0:HALF]).then_inc(sem.cp0, 1)
    g.vector.wait_ge(sem.mm1, 1)
    g.vector.tensor_copy(T.out[:, HALF:XW], T.acc1[:, 0:HALF]).then_inc(sem.cp1, 1)

    g.sync.wait_ge(sem.cp0, 1)
    g.sync.dma_start(T.y[:, 0:HALF], T.out[:, 0:HALF]).then_inc(sem.st0, 16)
    g.sync.wait_ge(sem.st0, 16)
    g.scalar.wait_ge(sem.cp1, 1)
    g.scalar.dma_start(T.y[:, HALF:XW], T.out[:, HALF:XW]).then_inc(sem.st1, 16)
    g.scalar.wait_ge(sem.st1, 16)

    g.wait_ge(sem.sent, sent)
